import numpy as np
import ml_dtypes


def mxq(x, axis, fmt="e4m3"):
    dtype, down = {"e4m3": (ml_dtypes.float8_e4m3fn, 7), "e5m2": (ml_dtypes.float8_e5m2, 14)}[fmt]
    v = np.moveaxis(np.asarray(x, np.float32).astype(ml_dtypes.bfloat16).astype(np.float64), axis, -1)
    blocks = v.reshape(v.shape[:-1] + (-1, 32))
    amax = np.abs(blocks).max(-1, keepdims=True)
    byte = np.maximum(np.where(amax > 0, np.frexp(amax)[1] - 1 + 127, 0) - down, 1)
    scale = np.exp2(byte - 127.0)
    codes = (blocks / scale).astype(np.float32).astype(dtype).astype(np.float64)
    return np.moveaxis((codes * scale).reshape(v.shape), -1, axis)


WIDE = False


def mx_kscale(k):
    if not WIDE:
        return np.ones(k)
    levels = np.array([10, -10, 5, -5, 0])
    if k % 512:
        return np.exp2(np.random.permutation(np.resize(levels, k // 32))).repeat(32)
    a = np.empty((k // 512, 16))
    for p in range(k // 512):
        a[p, :8] = np.random.permutation(np.resize(levels, 8))
        for g in range(8):
            far = levels[np.abs(levels - a[p, g]) >= 10]
            a[p, g + 8] = far[np.random.randint(len(far))]
    return np.exp2(a.ravel()).repeat(32)


def f64(x):
    return np.asarray(x).astype(np.float64)


def striped(idx):
    return np.tile(np.asarray(idx).reshape(-1, 16).T, (8, 1)).astype(np.uint16)


def unstriped(offs):
    return offs[:16].T.reshape(-1).astype(np.int64)


def striped8(idx):
    return np.asarray(idx).reshape(8, -1, 16).transpose(0, 2, 1).reshape(128, -1).astype(np.uint16)


def unstriped8(offs):
    return offs.reshape(8, 16, -1).transpose(0, 2, 1).reshape(8, -1).astype(np.int64)


def pick8(x, idx, run):
    r = np.arange(len(x))
    return x[r[:, None], idx[r % (8 * run) // run]]


E2M1 = np.array([0.0, 0.5, 1.0, 1.5, 2.0, 3.0, 4.0, 6.0, -0.0, -0.5, -1.0, -1.5, -2.0, -3.0, -4.0, -6.0])


def pack_weight(w, fmt):
    k, n = w.shape
    w = f64(np.asarray(w, np.float32).astype(ml_dtypes.bfloat16)).reshape(k // 32, 32, n)
    amax = np.abs(w).max(1)
    if fmt == "e4m3":
        byte = np.frexp(amax)[1] - 1 + 127 - 7
    else:
        mant, ex = np.frexp(amax / 6.0)
        byte = np.where(mant > 0.5, ex, ex - 1) + 127
    byte = np.clip(np.where(amax > 0, byte, 1), 1, 254)
    scaled = (w * np.exp2(127.0 - byte)[:, None, :]).reshape(k, n).astype(np.float32)
    by_word = np.ascontiguousarray(scaled.reshape(k // 512, 128, 4, n).transpose(0, 1, 3, 2))
    if fmt == "e4m3":
        words = by_word.astype(ml_dtypes.float8_e4m3fn).view(np.uint8)
    else:
        c = by_word.astype(ml_dtypes.float4_e2m1fn).view(np.uint8) & 0xF
        words = (c[..., 0::2] | (c[..., 1::2] << 4)).reshape(k // 512, 128, 2 * n)
    return np.ascontiguousarray(words), np.ascontiguousarray(byte.astype(np.uint8).reshape(k // 512, 16, n))


def unpack_weight(words, scales, fmt):
    g, _, n = scales.shape
    words = np.ascontiguousarray(words).reshape(g, 128, n, -1)
    if fmt == "e4m3":
        vals = words.view(ml_dtypes.float8_e4m3fn).astype(np.float64)
    else:
        nib = np.empty((g, 128, n, 4), np.uint8)
        nib[..., 0::2] = words & 0xF
        nib[..., 1::2] = words >> 4
        vals = E2M1[nib]
    vals = vals * np.repeat(np.exp2(scales.astype(np.float64) - 127.0), 8, axis=1)[..., None]
    return vals.transpose(0, 1, 3, 2).reshape(g * 512, n)


def sigmoid(v):
    return 1.0 / (1.0 + np.exp(-v))


def sgn(shape):
    return np.random.uniform(0.5, 2.0, shape) * np.where(np.random.standard_normal(shape) < 0, -1.0, 1.0)


K, T, J, R, S, O, U, E = 512, 1024, 256, 512, 1024, 256, 128, 256


def setup_inputs():
    n = np.random.standard_normal
    idx = np.random.permutation(T)[:J]
    idx2 = np.stack([np.random.permutation(S)[:O] for _ in range(8)])
    idx3 = np.random.permutation(J)[:U]
    idx4 = np.random.permutation(E)[:U]
    fk = mx_kscale(K)
    fr = mx_kscale(R)
    fr = fr / fr.max()
    xtp = pack_weight(n((K, T)) / fk[:, None], "e2m1")
    wp = pack_weight(n((K, R)) * 1 / np.sqrt(K) * fk[:, None], "e4m3")
    return {
        "xt_words": xtp[0],
        "xt_scales": xtp[1],
        "w_words": wp[0],
        "w_scales": wp[1],
        "en": (0.7 * n((R, S))).astype(np.float32),
        "sg": (0.4 * sgn((R, 1))).astype(np.float32),
        "lo": (np.random.uniform(-2.4, -1.0, (R, 1)) + np.log(fr)[:, None]).astype(np.float32),
        "sa": (sgn((R, 1)) / fr[:, None] / np.sqrt(R)).astype(np.float32),
        "so": (np.random.uniform(0.5, 1.6, (O, 1))).astype(np.float32),
        "offs": striped(idx),
        "offs2": striped8(idx2),
        "offs3": striped(idx3),
        "offs4": striped(idx4),
    }


def reference(xt_words, xt_scales, w_words, w_scales, en, sg, lo, sa, so, offs, offs2, offs3, offs4):
    idx = unstriped(offs)
    idx2 = unstriped8(offs2)
    idx3 = unstriped(offs3)
    idx4 = unstriped(offs4)
    xtu = unpack_weight(xt_words, xt_scales, "e2m1")
    wu = unpack_weight(w_words, w_scales, "e4m3")
    xtidxg = xtu[:, idx]
    a = wu.T @ xtidxg
    z1 = sigmoid(pick8(f64(en), idx2, 64) * f64(sg) + f64(lo))
    z2 = a[:, idx3] * f64(sa)
    z1q = mxq(z1, 0, "e4m3")
    z2q = mxq(z2, 0, "e4m3")
    p = z1q.T @ z2q
    y = np.zeros((O, E))
    y[:, idx4] = p * f64(so)
    return y

@@ -1,0 +1,143 @@
+from contextlib import ExitStack
+
+import concourse.mybir as mybir
+
+K, T, J, R, S, O, U, E = 512, 1024, 256, 512, 1024, 256, 128, 256
+FLOPS = 2 * K * R * J + 2 * R * O * U
+
+F32 = mybir.dt.float32
+BF16 = mybir.dt.bfloat16
+I32 = mybir.dt.int32
+U32 = mybir.dt.uint32
+U16 = mybir.dt.uint16
+U8 = mybir.dt.uint8
+FP8X4 = mybir.dt.float8_e4m3fn_x4
+FP4X4 = mybir.dt.float4_e2m1fn_x4
+ACT = mybir.ActivationFunctionType
+
+P = 128
+PACK = 4
+QUADS = 4
+KEY_PARTS = 2
+UH = U // KEY_PARTS
+OT = O // P
+
+
+def tile_list_memberscores_kernel(tc, xt_words, xt_scales, w_words, w_scales, en, sg, lo, sa, so,
+                                    offs, offs2, offs3, offs4, out):
+    nc = tc.nc
+    with ExitStack() as ctx:
+        sb = ctx.enter_context(tc.tile_pool(name="sb", bufs=1))
+        ps = ctx.enter_context(tc.psum_pool(name="ps", bufs=1))
+
+        def tile(shape, dtype, name):
+            return sb.tile(shape, dtype, name=name, align_bytes=64)
+
+        en_rows = en.rearrange("(p t) s -> t p s", t=PACK)
+        en_t = [tile([P, S], F32, "en%d" % t) for t in range(PACK)]
+        xw = tile([P, T], U16, "xw")
+        ww = tile([P, R], I32, "ww")
+        xs_stage = tile([PACK, QUADS, T // 4], I32, "xs_stage")
+        ws_stage = tile([P, QUADS, R // 4], I32, "ws_stage")
+        l1 = tile([P, J // 16], U16, "l1")
+        l2 = tile([P, O // 16], U16, "l2")
+        l3 = tile([P, U // 16], U16, "l3")
+        l4 = tile([P, U // 16], U16, "l4")
+        sg_t = tile([P, PACK], F32, "sg_t")
+        lo_t = tile([P, PACK], F32, "lo_t")
+        sa_t = tile([P, PACK], F32, "sa_t")
+        so_t = tile([P, OT], F32, "so_t")
+
+        ws_plane = tile([P, R], U8, "ws_plane")
+        xs_plane = tile([P, T], U8, "xs_plane")
+        pages = [tile([P, E], F32, "page%d" % h) for h in range(OT)]
+        nc.vector.memset(ws_stage[64:96], 0)
+        nc.vector.memset(xs_plane[:].bitcast(I32), 0)
+        for h in range(OT):
+            nc.vector.memset(pages[h][:], 0.0)
+
+        nc.sync.dma_start(en_t[0][:], en_rows[0])
+        nc.scalar.dma_start(sg_t[:], sg.rearrange("(p t) o -> p (t o)", t=PACK))
+        nc.scalar.dma_start(lo_t[:], lo.rearrange("(p t) o -> p (t o)", t=PACK))
+        nc.sync.dma_start(l2[:], offs2)
+        nc.sync.dma_start(xs_stage[:], xt_scales[0].bitcast(I32).rearrange("(q r) c -> r q c", r=PACK))
+        nc.sync.dma_start(ws_stage[64 : 64 + PACK], w_scales[0].bitcast(I32).rearrange("(q r) c -> r q c", r=PACK))
+        nc.sync.dma_start(l1[:], offs)
+        nc.sync.dma_start(en_t[1][:], en_rows[1])
+        nc.gpsimd.dma_start(sa_t[:], sa.rearrange("(p t) o -> p (t o)", t=PACK))
+        with nc.allow_non_contiguous_dma(reason="one value a partition for each tile of queries"):
+            nc.gpsimd.dma_start(so_t[:], so.rearrange("(h p) o -> p (h o)", p=P))
+        nc.sync.dma_start(xw[:].bitcast(I32), xt_words[0].bitcast(I32))
+        nc.sync.dma_start(en_t[2][:], en_rows[2])
+        nc.sync.dma_start(ww[:], w_words[0].rearrange("p c t -> p (c t)").bitcast(I32))
+        nc.sync.dma_start(l3[:], offs3)
+        nc.sync.dma_start(en_t[3][:], en_rows[3])
+        nc.sync.dma_start(l4[:], offs4)
+
+        for q in range(QUADS):
+            nc.vector.tensor_copy(xs_plane[32 * q : 32 * q + PACK, :].bitcast(I32), xs_stage[:, q, :])
+        for q in range(QUADS):
+            nc.vector.tensor_copy(ws_plane[32 * q : 32 * q + 32, :].bitcast(I32), ws_stage[64:96, q, :])
+        xs_g = tile([P, J], U8, "xs_g")
+        xw_g = tile([P, J], U16, "xw_g")
+        nc.vector.tensor_copy(xs_g[:], xs_plane[:].indirect(l1[:]))
+        nc.vector.tensor_copy(xw_g[:], xw[:].indirect(l1[:]))
+        ws_dealt = tile([P, R], U8, "ws_dealt")
+        nc.vector.tensor_copy(ws_dealt[:].rearrange("p (t m) -> p t m", t=PACK),
+                              ws_plane[:].rearrange("p (m t) -> p t m", t=PACK))
+
+        z1 = tile([P, PACK * O], BF16, "z1")
+        z2 = [tile([P, PACK * UH], BF16, "z2_%d" % g) for g in range(KEY_PARTS)]
+        a_t = [tile([P, J], F32, "a%d" % t) for t in range(PACK)]
+
+        def member(t):
+            nc.scalar.activation(out=z1[:, t : PACK * O : PACK], in_=en_t[t][:].indirect(l2[:]), func=ACT.Sigmoid,
+                                 bias=lo_t[:, t : t + 1], scale=sg_t[:, t : t + 1])
+
+        def value(g, t):
+            cols = UH // 16
+            nc.scalar.activation(out=z2[g][:, t : PACK * UH : PACK],
+                                 in_=a_t[t][:].indirect(l3[:, g * cols : (g + 1) * cols]),
+                                 func=ACT.Copy, scale=sa_t[:, t : t + 1])
+
+        for t in range(PACK - 1):
+            member(t)
+        ww_dealt = [tile([P, P], I32, "ww_dealt%d" % t) for t in range(PACK)]
+        for t in range(PACK):
+            nc.vector.tensor_copy(ww_dealt[t][:], ww[:, t:R:PACK])
+        for t in range(PACK):
+            acc = ps.tile([P, J], F32, name="acc%d" % t)
+            cols = slice(t * P, (t + 1) * P)
+            nc.tensor.matmul_mx(out=acc[:], lhsT=ww_dealt[t][:].bitcast(FP8X4), lhsT_scale=ws_dealt[:, cols],
+                                rhs=xw_g[:].bitcast(FP4X4), rhs_scale=xs_g[:], start=True, stop=True)
+            nc.vector.tensor_copy(a_t[t][:], acc[:])
+            value(0, t)
+        member(PACK - 1)
+        for t in range(PACK):
+            value(1, t)
+
+        z1c = [tile([P, P], U32, "z1c%d" % h) for h in range(OT)]
+        z1s = [tile([P, P], U8, "z1s%d" % h) for h in range(OT)]
+        z2c = [tile([P, UH], U32, "z2c%d" % g) for g in range(KEY_PARTS)]
+        z2s = [tile([P, UH], U8, "z2s%d" % g) for g in range(KEY_PARTS)]
+
+        def score(g, h):
+            acc = ps.tile([P, UH], F32, name="score%d_%d" % (g, h))
+            nc.tensor.matmul_mx(out=acc[:], lhsT=z1c[h][:].bitcast(FP8X4), lhsT_scale=z1s[h][:],
+                                rhs=z2c[g][:].bitcast(FP8X4), rhs_scale=z2s[g][:], start=True, stop=True)
+            p_sb = tile([P, UH], F32, "p%d_%d" % (g, h))
+            nc.vector.tensor_copy(p_sb[:], acc[:])
+            cols = UH // 16
+            nc.scalar.activation(out=pages[h][:].indirect(l4[:, g * cols : (g + 1) * cols]), in_=p_sb[:],
+                                 func=ACT.Copy, scale=so_t[:, h : h + 1])
+
+        nc.vector.quantize_mx(out=z2c[0][:].bitcast(FP8X4), scales=z2s[0][:], in_=z2[0][:])
+        for h in range(OT):
+            nc.vector.quantize_mx(out=z1c[h][:].bitcast(FP8X4), scales=z1s[h][:],
+                                  in_=z1[:, h * PACK * P : (h + 1) * PACK * P])
+        for h in range(OT):
+            score(0, h)
+        nc.vector.quantize_mx(out=z2c[1][:].bitcast(FP8X4), scales=z2s[1][:], in_=z2[1][:])
+        for h in range(OT):
+            score(1, h)
+            nc.sync.dma_start(out[h * P : (h + 1) * P, :], pages[h][:])

@@ -30,8 +30,8 @@ def tile_list_memberscores_kernel(tc, xt_words, xt_scales, w_words, w_scales, en
         sb = ctx.enter_context(tc.tile_pool(name="sb", bufs=1))
         ps = ctx.enter_context(tc.psum_pool(name="ps", bufs=1))
 
-        def tile(shape, dtype, name):
-            return sb.tile(shape, dtype, name=name, align_bytes=64)
+        def tile(shape, dtype, name, tag=None):
+            return sb.tile(shape, dtype, name=name, tag=tag or name, align_bytes=64)
 
         en_rows = en.rearrange("(p t) s -> t p s", t=PACK)
         en_t = [tile([P, S], F32, "en%d" % t) for t in range(PACK)]
@@ -58,33 +58,33 @@ def tile_list_memberscores_kernel(tc, xt_words, xt_scales, w_words, w_scales, en
 
         nc.sync.dma_start(en_t[0][:], en_rows[0])
         nc.scalar.dma_start(sg_t[:], sg.rearrange("(p t) o -> p (t o)", t=PACK))
-        nc.scalar.dma_start(lo_t[:], lo.rearrange("(p t) o -> p (t o)", t=PACK))
         nc.sync.dma_start(l2[:], offs2)
+        nc.scalar.dma_start(lo_t[:], lo.rearrange("(p t) o -> p (t o)", t=PACK))
         nc.sync.dma_start(xs_stage[:], xt_scales[0].bitcast(I32).rearrange("(q r) c -> r q c", r=PACK))
-        nc.sync.dma_start(ws_stage[64 : 64 + PACK], w_scales[0].bitcast(I32).rearrange("(q r) c -> r q c", r=PACK))
         nc.sync.dma_start(l1[:], offs)
         nc.sync.dma_start(en_t[1][:], en_rows[1])
-        nc.gpsimd.dma_start(sa_t[:], sa.rearrange("(p t) o -> p (t o)", t=PACK))
-        with nc.allow_non_contiguous_dma(reason="one value a partition for each tile of queries"):
-            nc.gpsimd.dma_start(so_t[:], so.rearrange("(h p) o -> p (h o)", p=P))
-        nc.sync.dma_start(xw[:].bitcast(I32), xt_words[0].bitcast(I32))
+        nc.sync.dma_start(ws_stage[64 : 64 + PACK], w_scales[0].bitcast(I32).rearrange("(q r) c -> r q c", r=PACK))
         nc.sync.dma_start(en_t[2][:], en_rows[2])
+        nc.sync.dma_start(xw[:].bitcast(I32), xt_words[0].bitcast(I32))
         nc.sync.dma_start(ww[:], w_words[0].rearrange("p c t -> p (c t)").bitcast(I32))
         nc.sync.dma_start(l3[:], offs3)
         nc.sync.dma_start(en_t[3][:], en_rows[3])
+        nc.sync.dma_start(sa_t[:], sa.rearrange("(p t) o -> p (t o)", t=PACK))
         nc.sync.dma_start(l4[:], offs4)
+        with nc.allow_non_contiguous_dma(reason="one value a partition for each tile of queries"):
+            nc.sync.dma_start(so_t[:], so.rearrange("(h p) o -> p (h o)", p=P))
 
         for q in range(QUADS):
             nc.vector.tensor_copy(xs_plane[32 * q : 32 * q + PACK, :].bitcast(I32), xs_stage[:, q, :])
-        for q in range(QUADS):
-            nc.vector.tensor_copy(ws_plane[32 * q : 32 * q + 32, :].bitcast(I32), ws_stage[64:96, q, :])
         xs_g = tile([P, J], U8, "xs_g")
         xw_g = tile([P, J], U16, "xw_g")
         nc.vector.tensor_copy(xs_g[:], xs_plane[:].indirect(l1[:]))
-        nc.vector.tensor_copy(xw_g[:], xw[:].indirect(l1[:]))
+        for q in range(QUADS):
+            nc.vector.tensor_copy(ws_plane[32 * q : 32 * q + 32, :].bitcast(I32), ws_stage[64:96, q, :])
         ws_dealt = tile([P, R], U8, "ws_dealt")
         nc.vector.tensor_copy(ws_dealt[:].rearrange("p (t m) -> p t m", t=PACK),
                               ws_plane[:].rearrange("p (m t) -> p t m", t=PACK))
+        nc.vector.tensor_copy(xw_g[:], xw[:].indirect(l1[:]))
 
         z1 = tile([P, PACK * O], BF16, "z1")
         z2 = [tile([P, PACK * UH], BF16, "z2_%d" % g) for g in range(KEY_PARTS)]
@@ -100,7 +100,7 @@ def tile_list_memberscores_kernel(tc, xt_words, xt_scales, w_words, w_scales, en
                                  in_=a_t[t][:].indirect(l3[:, g * cols : (g + 1) * cols]),
                                  func=ACT.Copy, scale=sa_t[:, t : t + 1])
 
-        for t in range(PACK - 1):
+        for t in range(PACK):
             member(t)
         ww_dealt = [tile([P, P], I32, "ww_dealt%d" % t) for t in range(PACK)]
         for t in range(PACK):
@@ -112,12 +112,14 @@ def tile_list_memberscores_kernel(tc, xt_words, xt_scales, w_words, w_scales, en
                                 rhs=xw_g[:].bitcast(FP4X4), rhs_scale=xs_g[:], start=True, stop=True)
             nc.vector.tensor_copy(a_t[t][:], acc[:])
             value(0, t)
-        member(PACK - 1)
+        z1c = [tile([P, P], U32, "z1c%d" % h) for h in range(OT)]
+        z1s = [tile([P, P], U8, "z1s%d" % h, tag) for h, tag in enumerate(("xs_g", "ws_dealt"))]
+        for h in range(OT):
+            nc.vector.quantize_mx(out=z1c[h][:].bitcast(FP8X4), scales=z1s[h][:],
+                                  in_=z1[:, h * PACK * P : (h + 1) * PACK * P])
         for t in range(PACK):
             value(1, t)
 
-        z1c = [tile([P, P], U32, "z1c%d" % h) for h in range(OT)]
-        z1s = [tile([P, P], U8, "z1s%d" % h) for h in range(OT)]
         z2c = [tile([P, UH], U32, "z2c%d" % g) for g in range(KEY_PARTS)]
         z2s = [tile([P, UH], U8, "z2s%d" % g) for g in range(KEY_PARTS)]
 
@@ -132,9 +134,6 @@ def tile_list_memberscores_kernel(tc, xt_words, xt_scales, w_words, w_scales, en
                                  func=ACT.Copy, scale=so_t[:, h : h + 1])
 
         nc.vector.quantize_mx(out=z2c[0][:].bitcast(FP8X4), scales=z2s[0][:], in_=z2[0][:])
-        for h in range(OT):
-            nc.vector.quantize_mx(out=z1c[h][:].bitcast(FP8X4), scales=z1s[h][:],
-                                  in_=z1[:, h * PACK * P : (h + 1) * PACK * P])
         for h in range(OT):
             score(0, h)
         nc.vector.quantize_mx(out=z2c[1][:].bitcast(FP8X4), scales=z2s[1][:], in_=z2[1][:])

@@ -38,7 +38,6 @@ def tile_list_memberscores_kernel(tc, xt_words, xt_scales, w_words, w_scales, en
         xw = tile([P, T], U16, "xw")
         ww = tile([P, R], I32, "ww")
         xs_stage = tile([PACK, QUADS, T // 4], I32, "xs_stage")
-        ws_stage = tile([P, QUADS, R // 4], I32, "ws_stage")
         l1 = tile([P, J // 16], U16, "l1")
         l2 = tile([P, O // 16], U16, "l2")
         l3 = tile([P, U // 16], U16, "l3")
@@ -48,27 +47,29 @@ def tile_list_memberscores_kernel(tc, xt_words, xt_scales, w_words, w_scales, en
         sa_t = tile([P, PACK], F32, "sa_t")
         so_t = tile([P, OT], F32, "so_t")
 
-        ws_plane = tile([P, R], U8, "ws_plane")
+        ws_plane = tile([P, 2, R], U8, "ws_plane")
         xs_plane = tile([P, T], U8, "xs_plane")
         pages = [tile([P, E], F32, "page%d" % h) for h in range(OT)]
-        nc.vector.memset(ws_stage[64:96], 0)
+        nc.vector.memset(ws_plane[:].bitcast(I32), 0)
         nc.vector.memset(xs_plane[:].bitcast(I32), 0)
         for h in range(OT):
             nc.vector.memset(pages[h][:], 0.0)
 
-        nc.sync.dma_start(en_t[0][:], en_rows[0])
         nc.scalar.dma_start(sg_t[:], sg.rearrange("(p t) o -> p (t o)", t=PACK))
+        nc.sync.dma_start(en_t[0][:], en_rows[0])
         nc.sync.dma_start(l2[:], offs2)
         nc.scalar.dma_start(lo_t[:], lo.rearrange("(p t) o -> p (t o)", t=PACK))
         nc.sync.dma_start(xs_stage[:], xt_scales[0].bitcast(I32).rearrange("(q r) c -> r q c", r=PACK))
         nc.sync.dma_start(l1[:], offs)
         nc.sync.dma_start(en_t[1][:], en_rows[1])
-        nc.sync.dma_start(ws_stage[64 : 64 + PACK], w_scales[0].bitcast(I32).rearrange("(q r) c -> r q c", r=PACK))
+        ws_rows = w_scales[0].bitcast(I32).rearrange("(b q r) c -> q r b c", b=2, r=PACK)
+        for q in range(2):
+            nc.sync.dma_start(ws_plane[64 + 32 * q : 64 + 32 * q + PACK].bitcast(I32), ws_rows[q])
         nc.sync.dma_start(en_t[2][:], en_rows[2])
         nc.sync.dma_start(xw[:].bitcast(I32), xt_words[0].bitcast(I32))
         nc.sync.dma_start(ww[:], w_words[0].rearrange("p c t -> p (c t)").bitcast(I32))
-        nc.sync.dma_start(l3[:], offs3)
         nc.sync.dma_start(en_t[3][:], en_rows[3])
+        nc.sync.dma_start(l3[:], offs3)
         nc.sync.dma_start(sa_t[:], sa.rearrange("(p t) o -> p (t o)", t=PACK))
         nc.sync.dma_start(l4[:], offs4)
         with nc.allow_non_contiguous_dma(reason="one value a partition for each tile of queries"):
@@ -79,11 +80,10 @@ def tile_list_memberscores_kernel(tc, xt_words, xt_scales, w_words, w_scales, en
         xs_g = tile([P, J], U8, "xs_g")
         xw_g = tile([P, J], U16, "xw_g")
         nc.vector.tensor_copy(xs_g[:], xs_plane[:].indirect(l1[:]))
-        for q in range(QUADS):
-            nc.vector.tensor_copy(ws_plane[32 * q : 32 * q + 32, :].bitcast(I32), ws_stage[64:96, q, :])
+        nc.vector.tensor_copy(ws_plane[0:64, 1, :].bitcast(I32), ws_plane[64:P, 0, :].bitcast(I32))
         ws_dealt = tile([P, R], U8, "ws_dealt")
         nc.vector.tensor_copy(ws_dealt[:].rearrange("p (t m) -> p t m", t=PACK),
-                              ws_plane[:].rearrange("p (m t) -> p t m", t=PACK))
+                              ws_plane[:, 1, :].rearrange("p (m t) -> p t m", t=PACK))
         nc.vector.tensor_copy(xw_g[:], xw[:].indirect(l1[:]))
 
         z1 = tile([P, PACK * O], BF16, "z1")

@@ -17,10 +17,16 @@ ACT = mybir.ActivationFunctionType
 
 P = 128
 PACK = 4
-QUADS = 4
-KEY_PARTS = 2
-UH = U // KEY_PARTS
-OT = O // P
+QUAD = 32
+QUADS = P // QUAD
+LIVE = 4
+HALF = P // 2
+WORD = 4
+LINE = 4
+LIST = 16
+KEY_HALVES = 2
+KEYS = U // KEY_HALVES
+QUERY_TILES = O // P
 
 
 def tile_list_memberscores_kernel(tc, xt_words, xt_scales, w_words, w_scales, en, sg, lo, sa, so,
@@ -37,36 +43,36 @@ def tile_list_memberscores_kernel(tc, xt_words, xt_scales, w_words, w_scales, en
         en_t = [tile([P, S], F32, "en%d" % t) for t in range(PACK)]
         xw = tile([P, T], U16, "xw")
         ww = tile([P, R], I32, "ww")
-        xs_stage = tile([PACK, QUADS, T // 4], I32, "xs_stage")
-        l1 = tile([P, J // 16], U16, "l1")
-        l2 = tile([P, O // 16], U16, "l2")
-        l3 = tile([P, U // 16], U16, "l3")
-        l4 = tile([P, U // 16], U16, "l4")
+        xs_stage = tile([LIVE, QUADS, T // WORD], I32, "xs_stage")
+        l1 = tile([P, J // LIST], U16, "l1")
+        l2 = tile([P, O // LIST], U16, "l2")
+        l3 = tile([P, U // LIST], U16, "l3")
+        l4 = tile([P, U // LIST], U16, "l4")
         sg_t = tile([P, PACK], F32, "sg_t")
         lo_t = tile([P, PACK], F32, "lo_t")
         sa_t = tile([P, PACK], F32, "sa_t")
-        so_t = tile([P, OT], F32, "so_t")
+        so_t = tile([P, QUERY_TILES], F32, "so_t")
 
         ws_plane = tile([P, 2, R], U8, "ws_plane")
         xs_plane = tile([P, T], U8, "xs_plane")
-        pages = [tile([P, E], F32, "page%d" % h) for h in range(OT)]
+        pages = [tile([P, E], F32, "page%d" % h) for h in range(QUERY_TILES)]
         nc.vector.memset(ws_plane[:].bitcast(I32), 0)
         nc.vector.memset(xs_plane[:].bitcast(I32), 0)
-        for h in range(OT):
+        for h in range(QUERY_TILES):
             nc.vector.memset(pages[h][:], 0.0)
 
         nc.scalar.dma_start(sg_t[:], sg.rearrange("(p t) o -> p (t o)", t=PACK))
+        nc.sync.dma_start(xs_stage[:], xt_scales[0].bitcast(I32).rearrange("(q i) c -> i q c", i=LIVE))
         nc.sync.dma_start(en_t[0][:], en_rows[0])
         nc.sync.dma_start(l2[:], offs2)
         nc.scalar.dma_start(lo_t[:], lo.rearrange("(p t) o -> p (t o)", t=PACK))
-        nc.sync.dma_start(xs_stage[:], xt_scales[0].bitcast(I32).rearrange("(q r) c -> r q c", r=PACK))
         nc.sync.dma_start(l1[:], offs)
         nc.sync.dma_start(en_t[1][:], en_rows[1])
-        ws_rows = w_scales[0].bitcast(I32).rearrange("(b q r) c -> q r b c", b=2, r=PACK)
-        for q in range(2):
-            nc.sync.dma_start(ws_plane[64 + 32 * q : 64 + 32 * q + PACK].bitcast(I32), ws_rows[q])
-        nc.sync.dma_start(en_t[2][:], en_rows[2])
+        ws_rows = w_scales[0].bitcast(I32).rearrange("(b q i) c -> q i b c", b=2, i=LIVE)
+        for q in range(QUADS // 2):
+            nc.sync.dma_start(ws_plane[HALF + QUAD * q : HALF + QUAD * q + LIVE].bitcast(I32), ws_rows[q])
         nc.sync.dma_start(xw[:].bitcast(I32), xt_words[0].bitcast(I32))
+        nc.sync.dma_start(en_t[2][:], en_rows[2])
         nc.sync.dma_start(ww[:], w_words[0].rearrange("p c t -> p (c t)").bitcast(I32))
         nc.sync.dma_start(en_t[3][:], en_rows[3])
         nc.sync.dma_start(l3[:], offs3)
@@ -76,67 +82,65 @@ def tile_list_memberscores_kernel(tc, xt_words, xt_scales, w_words, w_scales, en
             nc.sync.dma_start(so_t[:], so.rearrange("(h p) o -> p (h o)", p=P))
 
         for q in range(QUADS):
-            nc.vector.tensor_copy(xs_plane[32 * q : 32 * q + PACK, :].bitcast(I32), xs_stage[:, q, :])
+            nc.vector.tensor_copy(xs_plane[QUAD * q : QUAD * q + LIVE, :].bitcast(I32), xs_stage[:, q, :])
         xs_g = tile([P, J], U8, "xs_g")
         xw_g = tile([P, J], U16, "xw_g")
         nc.vector.tensor_copy(xs_g[:], xs_plane[:].indirect(l1[:]))
-        nc.vector.tensor_copy(ws_plane[0:64, 1, :].bitcast(I32), ws_plane[64:P, 0, :].bitcast(I32))
+        nc.vector.tensor_copy(ws_plane[0:HALF, 1, :].bitcast(I32), ws_plane[HALF:P, 0, :].bitcast(I32))
         ws_dealt = tile([P, R], U8, "ws_dealt")
         nc.vector.tensor_copy(ws_dealt[:].rearrange("p (t m) -> p t m", t=PACK),
                               ws_plane[:, 1, :].rearrange("p (m t) -> p t m", t=PACK))
         nc.vector.tensor_copy(xw_g[:], xw[:].indirect(l1[:]))
 
         z1 = tile([P, PACK * O], BF16, "z1")
-        z2 = [tile([P, PACK * UH], BF16, "z2_%d" % g) for g in range(KEY_PARTS)]
+        z2 = [tile([P, PACK * KEYS], BF16, "z2_%d" % g) for g in range(KEY_HALVES)]
         a_t = [tile([P, J], F32, "a%d" % t) for t in range(PACK)]
 
-        def member(t):
-            nc.scalar.activation(out=z1[:, t : PACK * O : PACK], in_=en_t[t][:].indirect(l2[:]), func=ACT.Sigmoid,
-                                 bias=lo_t[:, t : t + 1], scale=sg_t[:, t : t + 1])
+        def key_columns(g):
+            return slice(g * KEYS // LIST, (g + 1) * KEYS // LIST)
 
-        def value(g, t):
-            cols = UH // 16
-            nc.scalar.activation(out=z2[g][:, t : PACK * UH : PACK],
-                                 in_=a_t[t][:].indirect(l3[:, g * cols : (g + 1) * cols]),
+        def fetch_values(g, t):
+            nc.scalar.activation(out=z2[g][:, t : PACK * KEYS : PACK], in_=a_t[t][:].indirect(l3[:, key_columns(g)]),
                                  func=ACT.Copy, scale=sa_t[:, t : t + 1])
 
         for t in range(PACK):
-            member(t)
-        ww_dealt = [tile([P, P], I32, "ww_dealt%d" % t) for t in range(PACK)]
-        for t in range(PACK):
-            nc.vector.tensor_copy(ww_dealt[t][:], ww[:, t:R:PACK])
+            nc.scalar.activation(out=z1[:, t : PACK * O : PACK], in_=en_t[t][:].indirect(l2[:]), func=ACT.Sigmoid,
+                                 bias=lo_t[:, t : t + 1], scale=sg_t[:, t : t + 1])
+
+        ww_dealt = tile([P, R], I32, "ww_dealt")
+        nc.vector.tensor_copy(ww_dealt[:].rearrange("p (t c i) -> p c t i", t=PACK, i=LINE),
+                              ww[:].rearrange("p (c i t) -> p c t i", t=PACK, i=LINE))
         for t in range(PACK):
             acc = ps.tile([P, J], F32, name="acc%d" % t)
             cols = slice(t * P, (t + 1) * P)
-            nc.tensor.matmul_mx(out=acc[:], lhsT=ww_dealt[t][:].bitcast(FP8X4), lhsT_scale=ws_dealt[:, cols],
+            nc.tensor.matmul_mx(out=acc[:], lhsT=ww_dealt[:, cols].bitcast(FP8X4), lhsT_scale=ws_dealt[:, cols],
                                 rhs=xw_g[:].bitcast(FP4X4), rhs_scale=xs_g[:], start=True, stop=True)
             nc.vector.tensor_copy(a_t[t][:], acc[:])
-            value(0, t)
-        z1c = [tile([P, P], U32, "z1c%d" % h) for h in range(OT)]
-        z1s = [tile([P, P], U8, "z1s%d" % h, tag) for h, tag in enumerate(("xs_g", "ws_dealt"))]
-        for h in range(OT):
+            fetch_values(0, t)
+
+        z1c = [tile([P, P], U32, "z1c%d" % h) for h in range(QUERY_TILES)]
+        z1s = [tile([P, P], U8, "z1s%d" % h, tag) for h, tag in enumerate(("ww_dealt", "ws_dealt"))]
+        for h in range(QUERY_TILES):
             nc.vector.quantize_mx(out=z1c[h][:].bitcast(FP8X4), scales=z1s[h][:],
                                   in_=z1[:, h * PACK * P : (h + 1) * PACK * P])
         for t in range(PACK):
-            value(1, t)
+            fetch_values(1, t)
 
-        z2c = [tile([P, UH], U32, "z2c%d" % g) for g in range(KEY_PARTS)]
-        z2s = [tile([P, UH], U8, "z2s%d" % g) for g in range(KEY_PARTS)]
+        z2c = [tile([P, KEYS], U32, "z2c%d" % g) for g in range(KEY_HALVES)]
+        z2s = [tile([P, KEYS], U8, "z2s%d" % g) for g in range(KEY_HALVES)]
 
         def score(g, h):
-            acc = ps.tile([P, UH], F32, name="score%d_%d" % (g, h))
-            nc.tensor.matmul_mx(out=acc[:], lhsT=z1c[h][:].bitcast(FP8X4), lhsT_scale=z1s[h][:],
+            scores = ps.tile([P, KEYS], F32, name="score%d_%d" % (g, h))
+            nc.tensor.matmul_mx(out=scores[:], lhsT=z1c[h][:].bitcast(FP8X4), lhsT_scale=z1s[h][:],
                                 rhs=z2c[g][:].bitcast(FP8X4), rhs_scale=z2s[g][:], start=True, stop=True)
-            p_sb = tile([P, UH], F32, "p%d_%d" % (g, h))
-            nc.vector.tensor_copy(p_sb[:], acc[:])
-            cols = UH // 16
-            nc.scalar.activation(out=pages[h][:].indirect(l4[:, g * cols : (g + 1) * cols]), in_=p_sb[:],
+            p_sb = tile([P, KEYS], F32, "p%d_%d" % (g, h))
+            nc.vector.tensor_copy(p_sb[:], scores[:])
+            nc.scalar.activation(out=pages[h][:].indirect(l4[:, key_columns(g)]), in_=p_sb[:],
                                  func=ACT.Copy, scale=so_t[:, h : h + 1])
 
-        nc.vector.quantize_mx(out=z2c[0][:].bitcast(FP8X4), scales=z2s[0][:], in_=z2[0][:])
-        for h in range(OT):
-            score(0, h)
-        nc.vector.quantize_mx(out=z2c[1][:].bitcast(FP8X4), scales=z2s[1][:], in_=z2[1][:])
-        for h in range(OT):
-            score(1, h)
-            nc.sync.dma_start(out[h * P : (h + 1) * P, :], pages[h][:])
+        for g in range(KEY_HALVES):
+            nc.vector.quantize_mx(out=z2c[g][:].bitcast(FP8X4), scales=z2s[g][:], in_=z2[g][:])
+            for h in range(QUERY_TILES):
+                score(g, h)
+                if g == KEY_HALVES - 1:
+                    nc.sync.dma_start(out[h * P : (h + 1) * P, :], pages[h][:])

from contextlib import ExitStack

import concourse.mybir as mybir

K, T, J, R, S, O, U, E = 512, 1024, 256, 512, 1024, 256, 128, 256
FLOPS = 2 * K * R * J + 2 * R * O * U

F32 = mybir.dt.float32
BF16 = mybir.dt.bfloat16
I32 = mybir.dt.int32
U32 = mybir.dt.uint32
U16 = mybir.dt.uint16
U8 = mybir.dt.uint8
FP8X4 = mybir.dt.float8_e4m3fn_x4
FP4X4 = mybir.dt.float4_e2m1fn_x4
ACT = mybir.ActivationFunctionType

P = 128
PACK = 4
QUAD = 32
QUADS = P // QUAD
LIVE = 4
HALF = P // 2
WORD = 4
LINE = 4
LIST = 16
KEY_HALVES = 2
KEYS = U // KEY_HALVES
QUERY_TILES = O // P


def tile_list_memberscores_kernel(tc, xt_words, xt_scales, w_words, w_scales, en, sg, lo, sa, so,
                                    offs, offs2, offs3, offs4, out):
    nc = tc.nc
    with ExitStack() as ctx:
        sb = ctx.enter_context(tc.tile_pool(name="sb", bufs=1))
        ps = ctx.enter_context(tc.psum_pool(name="ps", bufs=1))

        def tile(shape, dtype, name, tag=None):
            return sb.tile(shape, dtype, name=name, tag=tag or name, align_bytes=64)

        en_rows = en.rearrange("(p t) s -> t p s", t=PACK)
        en_t = [tile([P, S], F32, "en%d" % t) for t in range(PACK)]
        xw = tile([P, T], U16, "xw")
        ww = tile([P, R], I32, "ww")
        xs_stage = tile([LIVE, QUADS, T // WORD], I32, "xs_stage")
        l1 = tile([P, J // LIST], U16, "l1")
        l2 = tile([P, O // LIST], U16, "l2")
        l3 = tile([P, U // LIST], U16, "l3")
        l4 = tile([P, U // LIST], U16, "l4")
        sg_t = tile([P, PACK], F32, "sg_t")
        lo_t = tile([P, PACK], F32, "lo_t")
        sa_t = tile([P, PACK], F32, "sa_t")
        so_t = tile([P, QUERY_TILES], F32, "so_t")

        ws_plane = tile([P, 2, R], U8, "ws_plane")
        xs_plane = tile([P, T], U8, "xs_plane")
        pages = [tile([P, E], F32, "page%d" % h) for h in range(QUERY_TILES)]
        nc.vector.memset(ws_plane[:].bitcast(I32), 0)
        nc.vector.memset(xs_plane[:].bitcast(I32), 0)
        for h in range(QUERY_TILES):
            nc.vector.memset(pages[h][:], 0.0)

        nc.scalar.dma_start(sg_t[:], sg.rearrange("(p t) o -> p (t o)", t=PACK))
        nc.sync.dma_start(xs_stage[:], xt_scales[0].bitcast(I32).rearrange("(q i) c -> i q c", i=LIVE))
        nc.sync.dma_start(en_t[0][:], en_rows[0])
        nc.sync.dma_start(l2[:], offs2)
        nc.scalar.dma_start(lo_t[:], lo.rearrange("(p t) o -> p (t o)", t=PACK))
        nc.sync.dma_start(l1[:], offs)
        nc.sync.dma_start(en_t[1][:], en_rows[1])
        ws_rows = w_scales[0].bitcast(I32).rearrange("(b q i) c -> q i b c", b=2, i=LIVE)
        for q in range(QUADS // 2):
            nc.sync.dma_start(ws_plane[HALF + QUAD * q : HALF + QUAD * q + LIVE].bitcast(I32), ws_rows[q])
        nc.sync.dma_start(xw[:].bitcast(I32), xt_words[0].bitcast(I32))
        nc.sync.dma_start(en_t[2][:], en_rows[2])
        nc.sync.dma_start(ww[:], w_words[0].rearrange("p c t -> p (c t)").bitcast(I32))
        nc.sync.dma_start(en_t[3][:], en_rows[3])
        nc.sync.dma_start(l3[:], offs3)
        nc.sync.dma_start(sa_t[:], sa.rearrange("(p t) o -> p (t o)", t=PACK))
        nc.sync.dma_start(l4[:], offs4)
        with nc.allow_non_contiguous_dma(reason="one value a partition for each tile of queries"):
            nc.sync.dma_start(so_t[:], so.rearrange("(h p) o -> p (h o)", p=P))

        for q in range(QUADS):
            nc.vector.tensor_copy(xs_plane[QUAD * q : QUAD * q + LIVE, :].bitcast(I32), xs_stage[:, q, :])
        xs_g = tile([P, J], U8, "xs_g")
        xw_g = tile([P, J], U16, "xw_g")
        nc.vector.tensor_copy(xs_g[:], xs_plane[:].indirect(l1[:]))
        nc.vector.tensor_copy(ws_plane[0:HALF, 1, :].bitcast(I32), ws_plane[HALF:P, 0, :].bitcast(I32))
        ws_dealt = tile([P, R], U8, "ws_dealt")
        nc.vector.tensor_copy(ws_dealt[:].rearrange("p (t m) -> p t m", t=PACK),
                              ws_plane[:, 1, :].rearrange("p (m t) -> p t m", t=PACK))
        nc.vector.tensor_copy(xw_g[:], xw[:].indirect(l1[:]))

        z1 = tile([P, PACK * O], BF16, "z1")
        z2 = [tile([P, PACK * KEYS], BF16, "z2_%d" % g) for g in range(KEY_HALVES)]
        a_t = [tile([P, J], F32, "a%d" % t) for t in range(PACK)]

        def key_columns(g):
            return slice(g * KEYS // LIST, (g + 1) * KEYS // LIST)

        def fetch_values(g, t):
            nc.scalar.activation(out=z2[g][:, t : PACK * KEYS : PACK], in_=a_t[t][:].indirect(l3[:, key_columns(g)]),
                                 func=ACT.Copy, scale=sa_t[:, t : t + 1])

        for t in range(PACK):
            nc.scalar.activation(out=z1[:, t : PACK * O : PACK], in_=en_t[t][:].indirect(l2[:]), func=ACT.Sigmoid,
                                 bias=lo_t[:, t : t + 1], scale=sg_t[:, t : t + 1])

        ww_dealt = tile([P, R], I32, "ww_dealt")
        nc.vector.tensor_copy(ww_dealt[:].rearrange("p (t c i) -> p c t i", t=PACK, i=LINE),
                              ww[:].rearrange("p (c i t) -> p c t i", t=PACK, i=LINE))
        for t in range(PACK):
            acc = ps.tile([P, J], F32, name="acc%d" % t)
            cols = slice(t * P, (t + 1) * P)
            nc.tensor.matmul_mx(out=acc[:], lhsT=ww_dealt[:, cols].bitcast(FP8X4), lhsT_scale=ws_dealt[:, cols],
                                rhs=xw_g[:].bitcast(FP4X4), rhs_scale=xs_g[:], start=True, stop=True)
            nc.vector.tensor_copy(a_t[t][:], acc[:])
            fetch_values(0, t)

        z1c = [tile([P, P], U32, "z1c%d" % h) for h in range(QUERY_TILES)]
        z1s = [tile([P, P], U8, "z1s%d" % h, tag) for h, tag in enumerate(("ww_dealt", "ws_dealt"))]
        for h in range(QUERY_TILES):
            nc.vector.quantize_mx(out=z1c[h][:].bitcast(FP8X4), scales=z1s[h][:],
                                  in_=z1[:, h * PACK * P : (h + 1) * PACK * P])
        for t in range(PACK):
            fetch_values(1, t)

        z2c = [tile([P, KEYS], U32, "z2c%d" % g) for g in range(KEY_HALVES)]
        z2s = [tile([P, KEYS], U8, "z2s%d" % g) for g in range(KEY_HALVES)]

        def score(g, h):
            scores = ps.tile([P, KEYS], F32, name="score%d_%d" % (g, h))
            nc.tensor.matmul_mx(out=scores[:], lhsT=z1c[h][:].bitcast(FP8X4), lhsT_scale=z1s[h][:],
                                rhs=z2c[g][:].bitcast(FP8X4), rhs_scale=z2s[g][:], start=True, stop=True)
            p_sb = tile([P, KEYS], F32, "p%d_%d" % (g, h))
            nc.vector.tensor_copy(p_sb[:], scores[:])
            nc.scalar.activation(out=pages[h][:].indirect(l4[:, key_columns(g)]), in_=p_sb[:],
                                 func=ACT.Copy, scale=so_t[:, h : h + 1])

        for g in range(KEY_HALVES):
            nc.vector.quantize_mx(out=z2c[g][:].bitcast(FP8X4), scales=z2s[g][:], in_=z2[g][:])
            for h in range(QUERY_TILES):
                score(g, h)
                if g == KEY_HALVES - 1:
                    nc.sync.dma_start(out[h * P : (h + 1) * P, :], pages[h][:])
